import numpy as np
import ml_dtypes


def mxq(x, axis, fmt="e4m3"):
    dtype, down = {"e4m3": (ml_dtypes.float8_e4m3fn, 7), "e5m2": (ml_dtypes.float8_e5m2, 14)}[fmt]
    v = np.moveaxis(np.asarray(x, np.float32).astype(ml_dtypes.bfloat16).astype(np.float64), axis, -1)
    blocks = v.reshape(v.shape[:-1] + (-1, 32))
    amax = np.abs(blocks).max(-1, keepdims=True)
    byte = np.maximum(np.where(amax > 0, np.frexp(amax)[1] - 1 + 127, 0) - down, 1)
    scale = np.exp2(byte - 127.0)
    codes = (blocks / scale).astype(np.float32).astype(dtype).astype(np.float64)
    return np.moveaxis((codes * scale).reshape(v.shape), -1, axis)


WIDE = False


def mx_kscale(k):
    if not WIDE:
        return np.ones(k)
    levels = np.array([10, -10, 5, -5, 0])
    if k % 512:
        return np.exp2(np.random.permutation(np.resize(levels, k // 32))).repeat(32)
    a = np.empty((k // 512, 16))
    for p in range(k // 512):
        a[p, :8] = np.random.permutation(np.resize(levels, 8))
        for g in range(8):
            far = levels[np.abs(levels - a[p, g]) >= 10]
            a[p, g + 8] = far[np.random.randint(len(far))]
    return np.exp2(a.ravel()).repeat(32)


BF16 = ml_dtypes.bfloat16


def bf(x):
    return np.asarray(x, np.float32).astype(BF16)


def f64(x):
    return np.asarray(x).astype(np.float64)


E2M1 = np.array([0.0, 0.5, 1.0, 1.5, 2.0, 3.0, 4.0, 6.0, -0.0, -0.5, -1.0, -1.5, -2.0, -3.0, -4.0, -6.0])


def pack_weight(w, fmt):
    k, n = w.shape
    w = f64(bf(w)).reshape(k // 32, 32, n)
    amax = np.abs(w).max(1)
    if fmt == "e4m3":
        byte = np.frexp(amax)[1] - 1 + 127 - 7
    else:
        mant, ex = np.frexp(amax / 6.0)
        byte = np.where(mant > 0.5, ex, ex - 1) + 127
    byte = np.clip(np.where(amax > 0, byte, 1), 1, 254)
    scaled = (w * np.exp2(127.0 - byte)[:, None, :]).reshape(k, n).astype(np.float32)
    by_word = np.ascontiguousarray(scaled.reshape(k // 512, 128, 4, n).transpose(0, 1, 3, 2))
    if fmt == "e4m3":
        words = by_word.astype(ml_dtypes.float8_e4m3fn).view(np.uint8)
    else:
        c = by_word.astype(ml_dtypes.float4_e2m1fn).view(np.uint8) & 0xF
        words = c[..., 0::2] | (c[..., 1::2] << 4)
    return np.ascontiguousarray(words), np.ascontiguousarray(byte.astype(np.uint8).reshape(k // 512, 16, n))


def unpack_weight(words, scales, fmt):
    g, p, n, _ = words.shape
    if fmt == "e4m3":
        vals = np.ascontiguousarray(words).view(ml_dtypes.float8_e4m3fn).astype(np.float64)
    else:
        nib = np.empty((g, p, n, 4), np.uint8)
        nib[..., 0::2] = words & 0xF
        nib[..., 1::2] = words >> 4
        vals = E2M1[nib]
    vals = vals * np.repeat(np.exp2(scales.astype(np.float64) - 127.0), 8, axis=1)[..., None]
    return vals.transpose(0, 1, 3, 2).reshape(g * 512, n)
def pack4(w):
    words, scales = pack_weight(w, "e2m1")
    return words.reshape(words.shape[0], 128, -1), scales


def unpack4(words, scales):
    return unpack_weight(words.reshape(words.shape[0], 128, -1, 2), scales, "e2m1")


K, C, N = 2048, 1024, 512


def setup_inputs():
    s = mx_kscale(K)
    energy = np.exp(1.5 * np.random.standard_normal((K, C)))
    taper = (1 + 0.1 * np.random.standard_normal(K)) * s
    low = np.random.standard_normal((K, N)) / np.sqrt(K) / s[:, None]
    band = np.random.standard_normal((K, N)) / np.sqrt(K) / s[:, None]
    gate = np.random.standard_normal((K, N)) / np.sqrt(K) / s[:, None]
    low_words, low_scales = pack4(low)
    band_words, band_scales = pack_weight(band, "e4m3")
    return {"energy": bf(energy), "taper": bf(taper),
            "low_words": low_words, "low_scales": low_scales,
            "band_words": band_words, "band_scales": band_scales,
            "gate": bf(gate), "bias": bf(0.3 * np.random.standard_normal(N))}


def reference(energy, taper, low_words, low_scales, band_words, band_scales, gate, bias):
    a = f64(energy) ** (1.0 / 3.0) * f64(taper)[:, None]
    aq = mxq(a, 0, "e4m3")
    slow = unpack4(low_words, low_scales).T @ aq
    fast = unpack_weight(band_words, band_scales, "e4m3").T @ aq
    z = mxq(f64(gate), 0, "e4m3").T @ aq
    gain = 1.0 / (1.0 + np.exp(-(z + f64(bias)[:, None])))
    return slow + gain * fast

@@ -1,0 +1,308 @@
+import math
+from contextlib import ExitStack
+
+import concourse.mybir as mybir
+
+K, C, N = 2048, 1024, 512
+FLOPS = 3 * 2 * K * C * N
+
+F32 = mybir.dt.float32
+BF16 = mybir.dt.bfloat16
+I32 = mybir.dt.int32
+U32 = mybir.dt.uint32
+U8 = mybir.dt.uint8
+FP8X4 = mybir.dt.float8_e4m3fn_x4
+FP4X4 = mybir.dt.float4_e2m1fn_x4
+ACT = mybir.ActivationFunctionType
+ALU = mybir.AluOpType
+
+P = 128
+PACK = 4
+PASSES = K // (P * PACK)
+HALF = 512
+HALVES = C // HALF
+NT = N // P
+BANKS = 8
+SHIFT = 30.0
+SHIFT_BITS = 43
+SIGN_AND_EXPONENT = -(1 << 23)
+MANTISSA = (1 << 23) - 1
+ONE_BITS = 127 << 23
+
+
+def tile_gammatone_modulation_filters_s10_kernel(
+    tc, energy, taper, low_words, low_scales, band_words, band_scales, gate, bias, out
+):
+    nc = tc.nc
+    with ExitStack() as ctx:
+        keep = ctx.enter_context(tc.tile_pool(name="keep", bufs=1))
+        work = ctx.enter_context(tc.tile_pool(name="work", bufs=3))
+        psum = ctx.enter_context(tc.psum_pool(name="psum", bufs=1))
+        ctx.enter_context(tc.manual_schedule())
+
+        def kept(shape, dtype, name):
+            return keep.tile(shape, dtype, name=name, align_bytes=64)
+
+        energy_rows = energy.rearrange("(g p j) c -> g p j c", p=P, j=PACK)
+        gate_rows = gate.rearrange("(g p j) n -> g p j n", p=P, j=PACK)
+
+        row_pieces = [[(0, 1), (1, 2), (2, 4)]] + [[(0, 2), (2, 4)]] * (PASSES - 1)
+        raw = {}
+        for g in range(PASSES):
+            for j0, j1 in row_pieces[g]:
+                raw[g, j0] = kept([P, j1 - j0, C], BF16, "raw%d_%d" % (g, j0))
+        logs = [kept([P, PACK, C], F32, "logs%d" % g) for g in range(PASSES)]
+        gate_raw = [kept([P, PACK, N], BF16, "gate_raw%d" % g) for g in range(PASSES)]
+        gate_codes = [kept([P, N], U32, "gate_codes%d" % g) for g in range(PASSES)]
+        gate_plane = [kept([P, N], U8, "gate_plane%d" % g) for g in range(PASSES)]
+        band_codes = kept([P, PASSES, N], U32, "band_codes")
+        low_codes = kept([P, PASSES, 2 * N], U8, "low_codes")
+        band_plane = kept([P, PASSES, N], U8, "band_plane")
+        low_plane = kept([P, PASSES, N], U8, "low_plane")
+        a_codes = {}
+        a_plane = {}
+        for h in range(HALVES):
+            for g in range(PASSES):
+                a_codes[h, g] = kept([P, HALF], U32, "a_codes%d_%d" % (h, g))
+                a_plane[h, g] = kept([P, HALF], U8, "a_plane%d_%d" % (h, g))
+        taper_sb = kept([P, PASSES, PACK], BF16, "taper_sb")
+        taper_f32 = kept([P, PASSES * PACK], F32, "taper_f32")
+        taper_power = kept([P, PASSES * PACK], I32, "taper_power")
+        taper_mantissa = kept([P, PASSES * PACK], I32, "taper_mantissa")
+        shift = kept([P, 1], F32, "shift")
+        taper_log = kept([P, PASSES * PACK], F32, "taper_log")
+        taper_sign = kept([P, PASSES, PACK], BF16, "taper_sign")
+        bias_sb = kept([P, NT, 2], BF16, "bias_sb")
+        ones = kept([P, 1], F32, "ones")
+        warm = kept([P, 1], F32, "warm")
+
+        def load_energy(g, piece):
+            j0, j1 = row_pieces[g][piece]
+            nc.sync.dma_start(out=raw[g, j0][:], in_=energy_rows[g][:, j0:j1, :])
+
+        def load_gate(g):
+            nc.sync.dma_start(out=gate_raw[g][:], in_=gate_rows[g])
+
+        def load_plane(plane, scales):
+            rows = scales.bitcast(I32).rearrange("g (q r) n -> r q g n", r=4)
+            for r in range(4):
+                nc.sync.dma_start(out=plane[:].bitcast(I32)[r:P:32], in_=rows[r])
+
+        def take_log(g, piece):
+            j0, j1 = row_pieces[g][piece]
+            nc.scalar.activation(out=logs[g][:, j0:j1, :], in_=raw[g, j0][:], func=ACT.Ln)
+
+        def add_taper_log(g, j):
+            col = g * PACK + j
+            nc.vector.tensor_scalar(
+                out=logs[g][:, j, :], in0=logs[g][:, j, :], scalar1=1.0 / 3.0,
+                scalar2=taper_log[:, col : col + 1], op0=ALU.mult, op1=ALU.add,
+            )
+
+        gate_grouped = {}
+
+        def group_gate(g):
+            gate_grouped[g] = work.tile([P, N, PACK], BF16, name="gate_grouped", bufs=2, align_bytes=64)
+            nc.vector.tensor_copy(
+                out=gate_grouped[g][:].rearrange("p (c i) t -> p c t i", i=4),
+                in_=gate_raw[g][:].rearrange("p t (c i) -> p c t i", i=4),
+            )
+
+        def quantize_gate(g):
+            nc.vector.quantize_mx(
+                out=gate_codes[g][:].bitcast(FP8X4), scales=gate_plane[g][:],
+                in_=gate_grouped[g][:].rearrange("p n t -> p (n t)"),
+            )
+
+        pairs = {}
+        grouped = {}
+
+        def take_exp(h, g, c0, c1):
+            pairs[h, g, c0] = work.tile([P, 2, c1 - c0, 2], BF16, name="pairs", bufs=4, align_bytes=64)
+            nc.scalar.activation(
+                out=pairs[h, g, c0][:],
+                in_=logs[g][:, :, h * HALF + c0 : h * HALF + c1].rearrange("p (u e) c -> p u c e", e=2),
+                func=ACT.Sigmoid, bias=shift[:],
+            )
+
+        def group_a(h, g, c0, c1):
+            if c0 == 0:
+                grouped[h, g] = work.tile([P, HALF, PACK], BF16, name="grouped", bufs=2, align_bytes=64)
+            nc.vector.tensor_tensor(
+                out=grouped[h, g][:, c0:c1, :].rearrange("p c (u e) -> p c u e", e=2),
+                in0=pairs[h, g, c0][:].rearrange("p u c e -> p c u e"),
+                in1=taper_sign[:, g, :].rearrange("p (u e) -> p u e", e=2).unsqueeze(1).to_broadcast([P, c1 - c0, 2, 2]),
+                op=ALU.mult,
+            )
+
+        def quantize_a(h, g, c0, c1):
+            nc.vector.quantize_mx(
+                out=a_codes[h, g][:, c0:c1].bitcast(FP8X4), scales=a_plane[h, g][:, c0:c1],
+                in_=grouped[h, g][:, c0:c1, :].rearrange("p c t -> p (c t)"),
+            )
+
+        order = [(h, nt, kind) for h in range(HALVES) for nt in range(NT) for kind in ("z", "fast", "slow")]
+        sums = {}
+
+        def multiply(h, nt, kind, g):
+            if g == 0:
+                sums[h, nt, kind] = psum.tile([P, HALF], F32, name="bank%d" % (order.index((h, nt, kind)) % BANKS))
+            cols = slice(nt * P, (nt + 1) * P)
+            if kind == "z":
+                weights, plane = gate_codes[g][:, cols].bitcast(FP8X4), gate_plane[g][:, cols]
+            elif kind == "fast":
+                weights, plane = band_codes[:, g, cols].bitcast(FP8X4), band_plane[:, g, cols]
+            else:
+                weights, plane = low_codes[:, g, 2 * nt * P : 2 * (nt + 1) * P].bitcast(FP4X4), low_plane[:, g, cols]
+            nc.tensor.matmul_mx(
+                out=sums[h, nt, kind][:], lhsT=weights, lhsT_scale=plane,
+                rhs=a_codes[h, g][:].bitcast(FP8X4), rhs_scale=a_plane[h, g][:],
+                start=(g == 0), stop=(g == PASSES - 1),
+            )
+
+        def first_groups(h, g):
+            for key in order[h * 12 : h * 12 + BANKS]:
+                multiply(*key, g)
+
+        def whole_group(h, nt, kind):
+            for g in range(PASSES):
+                multiply(h, nt, kind, g)
+
+        tanhs = {}
+        gated = {}
+
+        def take_tanh(h, nt):
+            tanhs[h, nt] = work.tile([P, HALF], F32, name="tanh", bufs=3)
+            nc.scalar.activation(
+                out=tanhs[h, nt][:], in_=sums[h, nt, "z"][:], func=ACT.Sigmoid, bias=bias_sb[:, nt, 0:1],
+            )
+
+        def apply_gain(h, nt):
+            gated[h, nt] = work.tile([P, HALF], F32, name="gated", bufs=2)
+            nc.vector.tensor_tensor(
+                out=gated[h, nt][:], in0=tanhs[h, nt][:], in1=sums[h, nt, "fast"][:], op=ALU.mult
+            )
+
+        def finish(h, nt):
+            result = work.tile([P, HALF], F32, name="result", bufs=4)
+            nc.vector.tensor_tensor(out=result[:], in0=gated[h, nt][:], in1=sums[h, nt, "slow"][:], op=ALU.add)
+            nc.sync.dma_start(out=out[nt * P : (nt + 1) * P, h * HALF : (h + 1) * HALF], in_=result[:])
+
+        nc.scalar.dma_start(out=taper_sb[:], in_=taper.rearrange("(g p j) -> p g j", p=P, j=PACK))
+        nc.vector.memset(ones[:], 1.0)
+        nc.vector.memset(shift[:], -SHIFT)
+        nc.scalar.activation(out=warm[:], in_=ones[:], func=ACT.Ln)
+        nc.gpsimd.memset(band_plane[:].bitcast(I32), 0)
+        nc.gpsimd.memset(low_plane[:].bitcast(I32), 0)
+        for piece in range(3):
+            load_energy(0, piece)
+        load_energy(1, 0)
+        load_gate(0)
+        load_energy(1, 1)
+        load_gate(1)
+        load_energy(2, 0)
+        load_energy(2, 1)
+        load_gate(2)
+        load_energy(3, 0)
+        load_gate(3)
+        load_energy(3, 1)
+        nc.sync.dma_start(
+            out=band_codes[:].bitcast(I32), in_=band_words.rearrange("g p n t -> p g (n t)").bitcast(I32)
+        )
+        nc.sync.dma_start(out=low_codes[:].bitcast(I32), in_=low_words.rearrange("g p n -> p g n").bitcast(I32))
+        load_plane(band_plane, band_scales)
+        load_plane(low_plane, low_scales)
+        with nc.allow_non_contiguous_dma(reason="one bias value a partition"):
+            nc.sync.dma_start(out=bias_sb[:, :, 0], in_=bias.rearrange("(t p) -> p t", p=P))
+
+        nc.vector.tensor_copy(out=taper_f32[:], in_=taper_sb[:].rearrange("p g j -> p (g j)"))
+        nc.vector.tensor_scalar(
+            out=taper_mantissa[:], in0=taper_f32[:].bitcast(I32), scalar1=MANTISSA, scalar2=ONE_BITS,
+            op0=ALU.bitwise_and, op1=ALU.bitwise_or,
+        )
+        nc.vector.tensor_scalar(
+            out=taper_power[:], in0=taper_f32[:].bitcast(I32), scalar1=SIGN_AND_EXPONENT, scalar2=None,
+            op0=ALU.bitwise_and,
+        )
+        nc.vector.tensor_scalar(
+            out=taper_sign[:].rearrange("p g j -> p (g j)"), in0=taper_power[:].bitcast(F32),
+            scalar1=2.0**SHIFT_BITS, scalar2=None, op0=ALU.mult,
+        )
+
+        take_log(0, 0)
+        nc.scalar.activation(
+            out=taper_log[:], in_=taper_mantissa[:].bitcast(F32), func=ACT.Ln,
+            scale=math.e**SHIFT / 2.0**SHIFT_BITS,
+        )
+        take_log(0, 1)
+        take_log(0, 2)
+        for j in range(PACK):
+            add_taper_log(0, j)
+        group_gate(0)
+        for g in range(1, PASSES):
+            take_log(g, 0)
+            add_taper_log(g, 0)
+            add_taper_log(g, 1)
+            quantize_gate(g - 1)
+            group_gate(g)
+            take_log(g, 1)
+            add_taper_log(g, 2)
+            add_taper_log(g, 3)
+        quantize_gate(PASSES - 1)
+
+        for g in range(PASSES):
+            take_exp(0, g, 0, 256)
+            group_a(0, g, 0, 256)
+            take_exp(0, g, 256, 384)
+            group_a(0, g, 256, 384)
+            quantize_a(0, g, 0, 256)
+            take_exp(0, g, 384, 512)
+            group_a(0, g, 384, 512)
+            quantize_a(0, g, 256, 512)
+            first_groups(0, g)
+
+        take_exp(1, 0, 0, HALF)
+        group_a(1, 0, 0, HALF)
+        take_tanh(0, 0)
+        apply_gain(0, 0)
+        quantize_a(1, 0, 0, HALF)
+        finish(0, 0)
+        take_tanh(0, 1)
+        take_tanh(0, 2)
+        whole_group(0, 2, "slow")
+        whole_group(0, 3, "z")
+        whole_group(0, 3, "fast")
+        whole_group(0, 3, "slow")
+        apply_gain(0, 1)
+        take_exp(1, 1, 0, HALF)
+        apply_gain(0, 2)
+        finish(0, 1)
+        group_a(1, 1, 0, HALF)
+        finish(0, 2)
+        take_tanh(0, 3)
+        apply_gain(0, 3)
+        quantize_a(1, 1, 0, HALF)
+        finish(0, 3)
+        first_groups(1, 0)
+        first_groups(1, 1)
+        for g in range(2, PASSES):
+            take_exp(1, g, 0, HALF)
+            group_a(1, g, 0, HALF)
+            quantize_a(1, g, 0, HALF)
+            first_groups(1, g)
+        take_tanh(1, 0)
+        apply_gain(1, 0)
+        take_tanh(1, 1)
+        apply_gain(1, 1)
+        finish(1, 0)
+        take_tanh(1, 2)
+        finish(1, 1)
+        whole_group(1, 2, "slow")
+        whole_group(1, 3, "z")
+        apply_gain(1, 2)
+        take_tanh(1, 3)
+        whole_group(1, 3, "fast")
+        finish(1, 2)
+        whole_group(1, 3, "slow")
+        apply_gain(1, 3)
+        finish(1, 3)

@@ -46,16 +46,18 @@ def tile_gammatone_modulation_filters_s10_kernel(
         energy_rows = energy.rearrange("(g p j) c -> g p j c", p=P, j=PACK)
         gate_rows = gate.rearrange("(g p j) n -> g p j n", p=P, j=PACK)
 
-        row_pieces = [[(0, 1), (1, 2), (2, 4)]] + [[(0, 2), (2, 4)]] * (PASSES - 1)
+        whole = (0, C)
+        row_pieces = [[(0, 1, 0, HALF), (0, 1, HALF, C), (1, 2, *whole), (2, 3, *whole), (3, 4, *whole)]]
+        row_pieces += [[(0, 2, *whole), (2, 4, *whole)]] * (PASSES - 1)
         raw = {}
         for g in range(PASSES):
-            for j0, j1 in row_pieces[g]:
-                raw[g, j0] = kept([P, j1 - j0, C], BF16, "raw%d_%d" % (g, j0))
+            for piece, (j0, j1, c0, c1) in enumerate(row_pieces[g]):
+                raw[g, piece] = kept([P, j1 - j0, c1 - c0], BF16, "raw%d_%d" % (g, piece))
         logs = [kept([P, PACK, C], F32, "logs%d" % g) for g in range(PASSES)]
         gate_raw = [kept([P, PACK, N], BF16, "gate_raw%d" % g) for g in range(PASSES)]
         gate_codes = [kept([P, N], U32, "gate_codes%d" % g) for g in range(PASSES)]
         gate_plane = [kept([P, N], U8, "gate_plane%d" % g) for g in range(PASSES)]
-        band_codes = kept([P, PASSES, N], U32, "band_codes")
+        band_codes = [kept([P, N], U32, "band_codes%d" % g) for g in range(PASSES)]
         low_codes = kept([P, PASSES, 2 * N], U8, "low_codes")
         band_plane = kept([P, PASSES, N], U8, "band_plane")
         low_plane = kept([P, PASSES, N], U8, "low_plane")
@@ -70,15 +72,17 @@ def tile_gammatone_modulation_filters_s10_kernel(
         taper_power = kept([P, PASSES * PACK], I32, "taper_power")
         taper_mantissa = kept([P, PASSES * PACK], I32, "taper_mantissa")
         shift = kept([P, 1], F32, "shift")
-        taper_log = kept([P, PASSES * PACK], F32, "taper_log")
+        taper_square = kept([P, PASSES * PACK], F32, "taper_square")
+        taper_cube = kept([P, PASSES * PACK], F32, "taper_cube")
+        taper_log = kept([P, PACK], F32, "taper_log")
         taper_sign = kept([P, PASSES, PACK], BF16, "taper_sign")
         bias_sb = kept([P, NT, 2], BF16, "bias_sb")
         ones = kept([P, 1], F32, "ones")
         warm = kept([P, 1], F32, "warm")
 
         def load_energy(g, piece):
-            j0, j1 = row_pieces[g][piece]
-            nc.sync.dma_start(out=raw[g, j0][:], in_=energy_rows[g][:, j0:j1, :])
+            j0, j1, c0, c1 = row_pieces[g][piece]
+            nc.sync.dma_start(out=raw[g, piece][:], in_=energy_rows[g][:, j0:j1, c0:c1])
 
         def load_gate(g):
             nc.sync.dma_start(out=gate_raw[g][:], in_=gate_rows[g])
@@ -89,14 +93,21 @@ def tile_gammatone_modulation_filters_s10_kernel(
                 nc.sync.dma_start(out=plane[:].bitcast(I32)[r:P:32], in_=rows[r])
 
         def take_log(g, piece):
-            j0, j1 = row_pieces[g][piece]
-            nc.scalar.activation(out=logs[g][:, j0:j1, :], in_=raw[g, j0][:], func=ACT.Ln)
+            j0, j1, c0, c1 = row_pieces[g][piece]
+            nc.scalar.activation(out=logs[g][:, j0:j1, c0:c1], in_=raw[g, piece][:], func=ACT.Ln)
 
-        def add_taper_log(g, j):
-            col = g * PACK + j
+        def take_scaled_logs(g, piece):
+            j0, j1, c0, c1 = row_pieces[g][piece]
+            for j in range(j0, j1):
+                col = g * PACK + j
+                nc.scalar.activation(
+                    out=logs[g][:, j, :], in_=raw[g, piece][:, j - j0, :], func=ACT.Ln,
+                    scale=taper_cube[:, col : col + 1],
+                )
+
+        def add_taper_log(j):
             nc.vector.tensor_scalar(
-                out=logs[g][:, j, :], in0=logs[g][:, j, :], scalar1=1.0 / 3.0,
-                scalar2=taper_log[:, col : col + 1], op0=ALU.mult, op1=ALU.add,
+                out=logs[0][:, j, :], in0=logs[0][:, j, :], scalar1=taper_log[:, j : j + 1], scalar2=None, op0=ALU.add
             )
 
         gate_grouped = {}
@@ -122,14 +133,13 @@ def tile_gammatone_modulation_filters_s10_kernel(
             nc.scalar.activation(
                 out=pairs[h, g, c0][:],
                 in_=logs[g][:, :, h * HALF + c0 : h * HALF + c1].rearrange("p (u e) c -> p u c e", e=2),
-                func=ACT.Sigmoid, bias=shift[:],
+                func=ACT.Sigmoid, bias=shift[:], scale=1.0 / 3.0,
             )
 
         def group_a(h, g, c0, c1):
-            if c0 == 0:
-                grouped[h, g] = work.tile([P, HALF, PACK], BF16, name="grouped", bufs=2, align_bytes=64)
+            grouped[h, g, c0] = work.tile([P, c1 - c0, PACK], BF16, name="grouped", bufs=4, align_bytes=64)
             nc.vector.tensor_tensor(
-                out=grouped[h, g][:, c0:c1, :].rearrange("p c (u e) -> p c u e", e=2),
+                out=grouped[h, g, c0][:].rearrange("p c (u e) -> p c u e", e=2),
                 in0=pairs[h, g, c0][:].rearrange("p u c e -> p c u e"),
                 in1=taper_sign[:, g, :].rearrange("p (u e) -> p u e", e=2).unsqueeze(1).to_broadcast([P, c1 - c0, 2, 2]),
                 op=ALU.mult,
@@ -138,55 +148,70 @@ def tile_gammatone_modulation_filters_s10_kernel(
         def quantize_a(h, g, c0, c1):
             nc.vector.quantize_mx(
                 out=a_codes[h, g][:, c0:c1].bitcast(FP8X4), scales=a_plane[h, g][:, c0:c1],
-                in_=grouped[h, g][:, c0:c1, :].rearrange("p c t -> p (c t)"),
+                in_=grouped[h, g, c0][:].rearrange("p c t -> p (c t)"),
             )
 
-        order = [(h, nt, kind) for h in range(HALVES) for nt in range(NT) for kind in ("z", "fast", "slow")]
         sums = {}
 
-        def multiply(h, nt, kind, g):
-            if g == 0:
-                sums[h, nt, kind] = psum.tile([P, HALF], F32, name="bank%d" % (order.index((h, nt, kind)) % BANKS))
+        def open_bank(key, bank):
+            sums[key] = psum.tile([P, HALF], F32, name="bank%d" % bank)
+
+        def multiply(h, nt, kind, g, c0, c1, acc):
             cols = slice(nt * P, (nt + 1) * P)
             if kind == "z":
                 weights, plane = gate_codes[g][:, cols].bitcast(FP8X4), gate_plane[g][:, cols]
             elif kind == "fast":
-                weights, plane = band_codes[:, g, cols].bitcast(FP8X4), band_plane[:, g, cols]
+                weights, plane = band_codes[g][:, cols].bitcast(FP8X4), band_plane[:, g, cols]
             else:
                 weights, plane = low_codes[:, g, 2 * nt * P : 2 * (nt + 1) * P].bitcast(FP4X4), low_plane[:, g, cols]
             nc.tensor.matmul_mx(
-                out=sums[h, nt, kind][:], lhsT=weights, lhsT_scale=plane,
-                rhs=a_codes[h, g][:].bitcast(FP8X4), rhs_scale=a_plane[h, g][:],
+                out=acc, lhsT=weights, lhsT_scale=plane,
+                rhs=a_codes[h, g][:, c0:c1].bitcast(FP8X4), rhs_scale=a_plane[h, g][:, c0:c1],
                 start=(g == 0), stop=(g == PASSES - 1),
             )
 
-        def first_groups(h, g):
-            for key in order[h * 12 : h * 12 + BANKS]:
-                multiply(*key, g)
+        def gate_and_band_pass(h, g, c0, c1, kinds=("z", "fast")):
+            for kind in kinds:
+                for nt in range(NT):
+                    if g == 0 and c0 == 0:
+                        open_bank((h, nt, kind), (nt + (4 if (kind == "fast") != (h == 1) else 0)))
+                    multiply(h, nt, kind, g, c0, c1, sums[h, nt, kind][:, c0:c1])
 
-        def whole_group(h, nt, kind):
+        def slow_group(h, nt, c0, c1, bank):
+            open_bank((h, nt, "slow", c0), bank)
             for g in range(PASSES):
-                multiply(h, nt, kind, g)
+                multiply(h, nt, "slow", g, c0, c1, sums[h, nt, "slow", c0][:, : c1 - c0])
+
+        def make_a(h, g, c0, c1):
+            mid = (c0 + c1) // 2
+            take_exp(h, g, c0, mid)
+            group_a(h, g, c0, mid)
+            take_exp(h, g, mid, c1)
+            group_a(h, g, mid, c1)
+            quantize_a(h, g, c0, mid)
+            quantize_a(h, g, mid, c1)
 
         tanhs = {}
         gated = {}
 
         def take_tanh(h, nt):
-            tanhs[h, nt] = work.tile([P, HALF], F32, name="tanh", bufs=3)
+            tanhs[h, nt] = work.tile([P, HALF], F32, name="tanh", bufs=4)
             nc.scalar.activation(
                 out=tanhs[h, nt][:], in_=sums[h, nt, "z"][:], func=ACT.Sigmoid, bias=bias_sb[:, nt, 0:1],
             )
 
         def apply_gain(h, nt):
-            gated[h, nt] = work.tile([P, HALF], F32, name="gated", bufs=2)
+            gated[h, nt] = work.tile([P, HALF], F32, name="gated", bufs=4)
             nc.vector.tensor_tensor(
                 out=gated[h, nt][:], in0=tanhs[h, nt][:], in1=sums[h, nt, "fast"][:], op=ALU.mult
             )
 
-        def finish(h, nt):
-            result = work.tile([P, HALF], F32, name="result", bufs=4)
-            nc.vector.tensor_tensor(out=result[:], in0=gated[h, nt][:], in1=sums[h, nt, "slow"][:], op=ALU.add)
-            nc.sync.dma_start(out=out[nt * P : (nt + 1) * P, h * HALF : (h + 1) * HALF], in_=result[:])
+        def finish(h, nt, c0, c1, queue):
+            result = work.tile([P, c1 - c0], F32, name="result", bufs=8)
+            nc.vector.tensor_tensor(
+                out=result[:], in0=gated[h, nt][:, c0:c1], in1=sums[h, nt, "slow", c0][:, : c1 - c0], op=ALU.add
+            )
+            queue.dma_start(out=out[nt * P : (nt + 1) * P, h * HALF + c0 : h * HALF + c1], in_=result[:])
 
         nc.scalar.dma_start(out=taper_sb[:], in_=taper.rearrange("(g p j) -> p g j", p=P, j=PACK))
         nc.vector.memset(ones[:], 1.0)
@@ -194,23 +219,24 @@ def tile_gammatone_modulation_filters_s10_kernel(
         nc.scalar.activation(out=warm[:], in_=ones[:], func=ACT.Ln)
         nc.gpsimd.memset(band_plane[:].bitcast(I32), 0)
         nc.gpsimd.memset(low_plane[:].bitcast(I32), 0)
-        for piece in range(3):
+        for piece in range(5):
             load_energy(0, piece)
         load_energy(1, 0)
-        load_gate(0)
         load_energy(1, 1)
-        load_gate(1)
+        load_gate(0)
         load_energy(2, 0)
+        load_gate(1)
         load_energy(2, 1)
-        load_gate(2)
         load_energy(3, 0)
-        load_gate(3)
+        load_gate(2)
         load_energy(3, 1)
-        nc.sync.dma_start(
-            out=band_codes[:].bitcast(I32), in_=band_words.rearrange("g p n t -> p g (n t)").bitcast(I32)
-        )
-        nc.sync.dma_start(out=low_codes[:].bitcast(I32), in_=low_words.rearrange("g p n -> p g n").bitcast(I32))
+        load_gate(3)
         load_plane(band_plane, band_scales)
+        for g in range(PASSES):
+            nc.sync.dma_start(
+                out=band_codes[g][:].bitcast(I32), in_=band_words[g].rearrange("p n t -> p (n t)").bitcast(I32)
+            )
+        nc.sync.dma_start(out=low_codes[:].bitcast(I32), in_=low_words.rearrange("g p n -> p g n").bitcast(I32))
         load_plane(low_plane, low_scales)
         with nc.allow_non_contiguous_dma(reason="one bias value a partition"):
             nc.sync.dma_start(out=bias_sb[:, :, 0], in_=bias.rearrange("(t p) -> p t", p=P))
@@ -224,85 +250,90 @@ def tile_gammatone_modulation_filters_s10_kernel(
             out=taper_power[:], in0=taper_f32[:].bitcast(I32), scalar1=SIGN_AND_EXPONENT, scalar2=None,
             op0=ALU.bitwise_and,
         )
+        mantissa = taper_mantissa[:].bitcast(F32)
+        nc.vector.scalar_tensor_tensor(
+            out=taper_square[:], in0=mantissa, scalar=(math.e**SHIFT / 2.0**SHIFT_BITS) ** 3, in1=mantissa,
+            op0=ALU.mult, op1=ALU.mult,
+        )
         nc.vector.tensor_scalar(
             out=taper_sign[:].rearrange("p g j -> p (g j)"), in0=taper_power[:].bitcast(F32),
             scalar1=2.0**SHIFT_BITS, scalar2=None, op0=ALU.mult,
         )
 
-        take_log(0, 0)
-        nc.scalar.activation(
-            out=taper_log[:], in_=taper_mantissa[:].bitcast(F32), func=ACT.Ln,
-            scale=math.e**SHIFT / 2.0**SHIFT_BITS,
-        )
-        take_log(0, 1)
-        take_log(0, 2)
+        nc.vector.tensor_tensor(out=taper_cube[:], in0=taper_square[:], in1=mantissa, op=ALU.mult)
+
+        for piece in range(4):
+            take_log(0, piece)
+        nc.scalar.activation(out=taper_log[:], in_=taper_cube[:, :PACK], func=ACT.Ln)
+        take_log(0, 4)
         for j in range(PACK):
-            add_taper_log(0, j)
-        group_gate(0)
+            add_taper_log(j)
         for g in range(1, PASSES):
-            take_log(g, 0)
-            add_taper_log(g, 0)
-            add_taper_log(g, 1)
-            quantize_gate(g - 1)
-            group_gate(g)
-            take_log(g, 1)
-            add_taper_log(g, 2)
-            add_taper_log(g, 3)
-        quantize_gate(PASSES - 1)
-
+            take_scaled_logs(g, 0)
+            take_scaled_logs(g, 1)
         for g in range(PASSES):
-            take_exp(0, g, 0, 256)
-            group_a(0, g, 0, 256)
-            take_exp(0, g, 256, 384)
-            group_a(0, g, 256, 384)
-            quantize_a(0, g, 0, 256)
-            take_exp(0, g, 384, 512)
-            group_a(0, g, 384, 512)
-            quantize_a(0, g, 256, 512)
-            first_groups(0, g)
+            group_gate(g)
+            quantize_gate(g)
 
-        take_exp(1, 0, 0, HALF)
-        group_a(1, 0, 0, HALF)
+        for c0 in (0, 256):
+            for g in range(PASSES):
+                make_a(0, g, c0, c0 + 256)
+                gate_and_band_pass(0, g, c0, c0 + 256)
+
+        take_exp(1, 0, 0, 256)
+        group_a(1, 0, 0, 256)
         take_tanh(0, 0)
-        apply_gain(0, 0)
-        quantize_a(1, 0, 0, HALF)
-        finish(0, 0)
+        slow_group(0, 0, 0, HALF, 0)
         take_tanh(0, 1)
-        take_tanh(0, 2)
-        whole_group(0, 2, "slow")
-        whole_group(0, 3, "z")
-        whole_group(0, 3, "fast")
-        whole_group(0, 3, "slow")
+        slow_group(0, 1, 0, HALF, 1)
+        apply_gain(0, 0)
+        quantize_a(1, 0, 0, 256)
         apply_gain(0, 1)
-        take_exp(1, 1, 0, HALF)
-        apply_gain(0, 2)
-        finish(0, 1)
-        group_a(1, 1, 0, HALF)
-        finish(0, 2)
+        finish(0, 0, 0, HALF, nc.sync)
+        take_tanh(0, 2)
+        slow_group(0, 2, 0, HALF, 2)
+        take_exp(1, 1, 0, 256)
         take_tanh(0, 3)
+        slow_group(0, 3, 0, HALF, 3)
+        apply_gain(0, 2)
+        finish(0, 1, 0, HALF, nc.sync)
         apply_gain(0, 3)
-        quantize_a(1, 1, 0, HALF)
-        finish(0, 3)
-        first_groups(1, 0)
-        first_groups(1, 1)
-        for g in range(2, PASSES):
-            take_exp(1, g, 0, HALF)
-            group_a(1, g, 0, HALF)
-            quantize_a(1, g, 0, HALF)
-            first_groups(1, g)
-        take_tanh(1, 0)
-        apply_gain(1, 0)
-        take_tanh(1, 1)
-        apply_gain(1, 1)
-        finish(1, 0)
-        take_tanh(1, 2)
-        finish(1, 1)
-        whole_group(1, 2, "slow")
-        whole_group(1, 3, "z")
-        apply_gain(1, 2)
-        take_tanh(1, 3)
-        whole_group(1, 3, "fast")
-        finish(1, 2)
-        whole_group(1, 3, "slow")
-        apply_gain(1, 3)
-        finish(1, 3)
+        finish(0, 2, 0, HALF, nc.sync)
+        group_a(1, 1, 0, 256)
+        finish(0, 3, 0, HALF, nc.sync)
+        quantize_a(1, 1, 0, 256)
+        gate_and_band_pass(1, 0, 0, 256)
+        gate_and_band_pass(1, 1, 0, 256)
+        take_exp(1, 2, 0, 256)
+        group_a(1, 2, 0, 256)
+        take_exp(1, 3, 0, 256)
+        group_a(1, 3, 0, 256)
+        quantize_a(1, 2, 0, 256)
+        gate_and_band_pass(1, 2, 0, 256)
+        take_exp(1, 0, 256, 512)
+        group_a(1, 0, 256, 512)
+        quantize_a(1, 3, 0, 256)
+        gate_and_band_pass(1, 3, 0, 256)
+        take_exp(1, 1, 256, 512)
+        group_a(1, 1, 256, 512)
+        quantize_a(1, 0, 256, 512)
+        gate_and_band_pass(1, 0, 256, 512)
+        take_exp(1, 2, 256, 512)
+        group_a(1, 2, 256, 512)
+        quantize_a(1, 1, 256, 512)
+        gate_and_band_pass(1, 1, 256, 512)
+        take_exp(1, 3, 256, 512)
+        group_a(1, 3, 256, 512)
+        quantize_a(1, 2, 256, 512)
+        gate_and_band_pass(1, 2, 256, 512)
+        quantize_a(1, 3, 256, 512)
+        gate_and_band_pass(1, 3, 256, 512)
+        for nt in range(NT):
+            take_tanh(1, nt)
+            apply_gain(1, nt)
+        for nt in range(NT - 1):
+            slow_group(1, nt, 0, HALF, 4 + nt)
+            finish(1, nt, 0, HALF, nc.sync)
+        for i, bank in enumerate((7, 0, 1, 2)):
+            slow_group(1, NT - 1, i * P, (i + 1) * P, bank)
+            finish(1, NT - 1, i * P, (i + 1) * P, nc.scalar if i % 2 else nc.sync)

@@ -23,6 +23,8 @@ HALF = 512
 HALVES = C // HALF
 NT = N // P
 BANKS = 8
+WARM_UPS = 6
+LATE_ROW = (3, 2)
 SHIFT = 30.0
 SHIFT_BITS = 43
 SIGN_AND_EXPONENT = -(1 << 23)
@@ -74,7 +76,7 @@ def tile_gammatone_modulation_filters_s10_kernel(
         shift = kept([P, 1], F32, "shift")
         taper_square = kept([P, PASSES * PACK], F32, "taper_square")
         taper_cube = kept([P, PASSES * PACK], F32, "taper_cube")
-        taper_log = kept([P, PACK], F32, "taper_log")
+        taper_log = kept([P, PASSES * PACK], F32, "taper_log")
         taper_sign = kept([P, PASSES, PACK], BF16, "taper_sign")
         bias_sb = kept([P, NT, 2], BF16, "bias_sb")
         ones = kept([P, 1], F32, "ones")
@@ -102,12 +104,14 @@ def tile_gammatone_modulation_filters_s10_kernel(
                 col = g * PACK + j
                 nc.scalar.activation(
                     out=logs[g][:, j, :], in_=raw[g, piece][:, j - j0, :], func=ACT.Ln,
-                    scale=taper_cube[:, col : col + 1],
+                    scale=1.0 if (g, j) == LATE_ROW else taper_cube[:, col : col + 1],
                 )
 
-        def add_taper_log(j):
+        def add_taper_log(g, j):
+            col = g * PACK + j
             nc.vector.tensor_scalar(
-                out=logs[0][:, j, :], in0=logs[0][:, j, :], scalar1=taper_log[:, j : j + 1], scalar2=None, op0=ALU.add
+                out=logs[g][:, j, :], in0=logs[g][:, j, :], scalar1=taper_log[:, col : col + 1], scalar2=None,
+                op0=ALU.add,
             )
 
         gate_grouped = {}
@@ -264,16 +268,24 @@ def tile_gammatone_modulation_filters_s10_kernel(
 
         for piece in range(4):
             take_log(0, piece)
-        nc.scalar.activation(out=taper_log[:], in_=taper_cube[:, :PACK], func=ACT.Ln)
+        nc.scalar.activation(out=taper_log[:], in_=taper_cube[:], func=ACT.Ln)
         take_log(0, 4)
         for j in range(PACK):
-            add_taper_log(j)
+            add_taper_log(0, j)
         for g in range(1, PASSES):
             take_scaled_logs(g, 0)
             take_scaled_logs(g, 1)
         for g in range(PASSES):
             group_gate(g)
+            if g == PASSES - 1:
+                add_taper_log(*LATE_ROW)
             quantize_gate(g)
+        scratch = psum.tile([P, HALF], F32, name="bank7")
+        for i in range(WARM_UPS):
+            nc.tensor.matmul_mx(
+                out=scratch[:], lhsT=gate_codes[3][:, :P].bitcast(FP8X4), lhsT_scale=gate_plane[3][:, :P],
+                rhs=gate_codes[3][:].bitcast(FP8X4), rhs_scale=gate_plane[3][:], start=True, stop=True,
+            )
 
         for c0 in (0, 256):
             for g in range(PASSES):

@@ -19,17 +19,21 @@ ALU = mybir.AluOpType
 P = 128
 PACK = 4
 PASSES = K // (P * PACK)
+LAST_PASS = PASSES - 1
 HALF = 512
 HALVES = C // HALF
-NT = N // P
-BANKS = 8
-WARM_UPS = 6
-LATE_ROW = (3, 2)
+STAGE = HALF // 2
+TILES = N // P
+LAST_TILE = TILES - 1
+
 SHIFT = 30.0
 SHIFT_BITS = 43
 SIGN_AND_EXPONENT = -(1 << 23)
 MANTISSA = (1 << 23) - 1
 ONE_BITS = 127 << 23
+
+WARM_UPS = 6
+LATE_ROW = (LAST_PASS, PACK - 2)
 
 
 def tile_gammatone_modulation_filters_s10_kernel(
@@ -45,18 +49,17 @@ def tile_gammatone_modulation_filters_s10_kernel(
         def kept(shape, dtype, name):
             return keep.tile(shape, dtype, name=name, align_bytes=64)
 
-        energy_rows = energy.rearrange("(g p j) c -> g p j c", p=P, j=PACK)
-        gate_rows = gate.rearrange("(g p j) n -> g p j n", p=P, j=PACK)
+        energy_rows = energy.rearrange("(g p t) c -> g p t c", p=P, t=PACK)
+        gate_rows = gate.rearrange("(g p t) n -> g p t n", p=P, t=PACK)
 
-        whole = (0, C)
-        row_pieces = [[(0, 1, 0, HALF), (0, 1, HALF, C), (1, 2, *whole), (2, 3, *whole), (3, 4, *whole)]]
-        row_pieces += [[(0, 2, *whole), (2, 4, *whole)]] * (PASSES - 1)
-        raw = {}
+        pieces = [[(0, 1, 0, HALF), (0, 1, HALF, C)] + [(t, t + 1, 0, C) for t in range(1, PACK)]]
+        pieces += [[(0, 2, 0, C), (2, 4, 0, C)]] * (PASSES - 1)
+        energy_sb = {}
         for g in range(PASSES):
-            for piece, (j0, j1, c0, c1) in enumerate(row_pieces[g]):
-                raw[g, piece] = kept([P, j1 - j0, c1 - c0], BF16, "raw%d_%d" % (g, piece))
+            for i, (t0, t1, c0, c1) in enumerate(pieces[g]):
+                energy_sb[g, i] = kept([P, t1 - t0, c1 - c0], BF16, "energy%d_%d" % (g, i))
         logs = [kept([P, PACK, C], F32, "logs%d" % g) for g in range(PASSES)]
-        gate_raw = [kept([P, PACK, N], BF16, "gate_raw%d" % g) for g in range(PASSES)]
+        gate_sb = [kept([P, PACK, N], BF16, "gate%d" % g) for g in range(PASSES)]
         gate_codes = [kept([P, N], U32, "gate_codes%d" % g) for g in range(PASSES)]
         gate_plane = [kept([P, N], U8, "gate_plane%d" % g) for g in range(PASSES)]
         band_codes = [kept([P, N], U32, "band_codes%d" % g) for g in range(PASSES)]
@@ -73,86 +76,85 @@ def tile_gammatone_modulation_filters_s10_kernel(
         taper_f32 = kept([P, PASSES * PACK], F32, "taper_f32")
         taper_power = kept([P, PASSES * PACK], I32, "taper_power")
         taper_mantissa = kept([P, PASSES * PACK], I32, "taper_mantissa")
-        shift = kept([P, 1], F32, "shift")
+        minus_shift = kept([P, 1], F32, "minus_shift")
         taper_square = kept([P, PASSES * PACK], F32, "taper_square")
         taper_cube = kept([P, PASSES * PACK], F32, "taper_cube")
         taper_log = kept([P, PASSES * PACK], F32, "taper_log")
-        taper_sign = kept([P, PASSES, PACK], BF16, "taper_sign")
-        bias_sb = kept([P, NT, 2], BF16, "bias_sb")
-        ones = kept([P, 1], F32, "ones")
-        warm = kept([P, 1], F32, "warm")
+        taper_factor = kept([P, PASSES, PACK], BF16, "taper_factor")
+        bias_sb = kept([P, TILES, 2], BF16, "bias_sb")
 
-        def load_energy(g, piece):
-            j0, j1, c0, c1 = row_pieces[g][piece]
-            nc.sync.dma_start(out=raw[g, piece][:], in_=energy_rows[g][:, j0:j1, c0:c1])
+        def load_energy(g, i):
+            t0, t1, c0, c1 = pieces[g][i]
+            nc.sync.dma_start(out=energy_sb[g, i][:], in_=energy_rows[g][:, t0:t1, c0:c1])
 
         def load_gate(g):
-            nc.sync.dma_start(out=gate_raw[g][:], in_=gate_rows[g])
+            nc.sync.dma_start(out=gate_sb[g][:], in_=gate_rows[g])
 
         def load_plane(plane, scales):
             rows = scales.bitcast(I32).rearrange("g (q r) n -> r q g n", r=4)
             for r in range(4):
                 nc.sync.dma_start(out=plane[:].bitcast(I32)[r:P:32], in_=rows[r])
 
-        def take_log(g, piece):
-            j0, j1, c0, c1 = row_pieces[g][piece]
-            nc.scalar.activation(out=logs[g][:, j0:j1, c0:c1], in_=raw[g, piece][:], func=ACT.Ln)
+        def take_plain_log(g, i):
+            t0, t1, c0, c1 = pieces[g][i]
+            nc.scalar.activation(out=logs[g][:, t0:t1, c0:c1], in_=energy_sb[g, i][:], func=ACT.Ln)
 
-        def take_scaled_logs(g, piece):
-            j0, j1, c0, c1 = row_pieces[g][piece]
-            for j in range(j0, j1):
-                col = g * PACK + j
+        def take_tapered_logs(g, i):
+            t0, t1 = pieces[g][i][:2]
+            for t in range(t0, t1):
+                col = g * PACK + t
                 nc.scalar.activation(
-                    out=logs[g][:, j, :], in_=raw[g, piece][:, j - j0, :], func=ACT.Ln,
-                    scale=1.0 if (g, j) == LATE_ROW else taper_cube[:, col : col + 1],
+                    out=logs[g][:, t, :], in_=energy_sb[g, i][:, t - t0, :], func=ACT.Ln,
+                    scale=1.0 if (g, t) == LATE_ROW else taper_cube[:, col : col + 1],
                 )
 
-        def add_taper_log(g, j):
-            col = g * PACK + j
+        def add_taper_log(g, t):
+            col = g * PACK + t
             nc.vector.tensor_scalar(
-                out=logs[g][:, j, :], in0=logs[g][:, j, :], scalar1=taper_log[:, col : col + 1], scalar2=None,
+                out=logs[g][:, t, :], in0=logs[g][:, t, :], scalar1=taper_log[:, col : col + 1], scalar2=None,
                 op0=ALU.add,
             )
 
-        gate_grouped = {}
+        gate_packed = {}
 
-        def group_gate(g):
-            gate_grouped[g] = work.tile([P, N, PACK], BF16, name="gate_grouped", bufs=2, align_bytes=64)
+        def interleave_gate(g):
+            gate_packed[g] = work.tile([P, N, PACK], BF16, name="gate_packed", bufs=2, align_bytes=64)
             nc.vector.tensor_copy(
-                out=gate_grouped[g][:].rearrange("p (c i) t -> p c t i", i=4),
-                in_=gate_raw[g][:].rearrange("p t (c i) -> p c t i", i=4),
+                out=gate_packed[g][:].rearrange("p (n i) t -> p n t i", i=4),
+                in_=gate_sb[g][:].rearrange("p t (n i) -> p n t i", i=4),
             )
 
         def quantize_gate(g):
             nc.vector.quantize_mx(
                 out=gate_codes[g][:].bitcast(FP8X4), scales=gate_plane[g][:],
-                in_=gate_grouped[g][:].rearrange("p n t -> p (n t)"),
+                in_=gate_packed[g][:].rearrange("p n t -> p (n t)"),
             )
 
-        pairs = {}
-        grouped = {}
+        roots = {}
+        a_packed = {}
 
-        def take_exp(h, g, c0, c1):
-            pairs[h, g, c0] = work.tile([P, 2, c1 - c0, 2], BF16, name="pairs", bufs=4, align_bytes=64)
+        def take_roots(h, g, c0, c1):
+            roots[h, g, c0] = work.tile([P, 2, c1 - c0, 2], BF16, name="roots", bufs=4, align_bytes=64)
             nc.scalar.activation(
-                out=pairs[h, g, c0][:],
+                out=roots[h, g, c0][:],
                 in_=logs[g][:, :, h * HALF + c0 : h * HALF + c1].rearrange("p (u e) c -> p u c e", e=2),
-                func=ACT.Sigmoid, bias=shift[:], scale=1.0 / 3.0,
+                func=ACT.Sigmoid, bias=minus_shift[:], scale=1.0 / 3.0,
             )
 
-        def group_a(h, g, c0, c1):
-            grouped[h, g, c0] = work.tile([P, c1 - c0, PACK], BF16, name="grouped", bufs=4, align_bytes=64)
+        def pack_a(h, g, c0, c1):
+            a_packed[h, g, c0] = work.tile([P, c1 - c0, PACK], BF16, name="a_packed", bufs=4, align_bytes=64)
+            factor = taper_factor[:, g, :].rearrange("p (u e) -> p u e", e=2)
             nc.vector.tensor_tensor(
-                out=grouped[h, g, c0][:].rearrange("p c (u e) -> p c u e", e=2),
-                in0=pairs[h, g, c0][:].rearrange("p u c e -> p c u e"),
-                in1=taper_sign[:, g, :].rearrange("p (u e) -> p u e", e=2).unsqueeze(1).to_broadcast([P, c1 - c0, 2, 2]),
+                out=a_packed[h, g, c0][:].rearrange("p c (u e) -> p c u e", e=2),
+                in0=roots[h, g, c0][:].rearrange("p u c e -> p c u e"),
+                in1=factor.unsqueeze(1).to_broadcast([P, c1 - c0, 2, 2]),
                 op=ALU.mult,
             )
 
         def quantize_a(h, g, c0, c1):
             nc.vector.quantize_mx(
                 out=a_codes[h, g][:, c0:c1].bitcast(FP8X4), scales=a_plane[h, g][:, c0:c1],
-                in_=grouped[h, g, c0][:].rearrange("p c t -> p (c t)"),
+                in_=a_packed[h, g, c0][:].rearrange("p c t -> p (c t)"),
             )
 
         sums = {}
@@ -160,71 +162,61 @@ def tile_gammatone_modulation_filters_s10_kernel(
         def open_bank(key, bank):
             sums[key] = psum.tile([P, HALF], F32, name="bank%d" % bank)
 
-        def multiply(h, nt, kind, g, c0, c1, acc):
-            cols = slice(nt * P, (nt + 1) * P)
-            if kind == "z":
-                weights, plane = gate_codes[g][:, cols].bitcast(FP8X4), gate_plane[g][:, cols]
-            elif kind == "fast":
-                weights, plane = band_codes[g][:, cols].bitcast(FP8X4), band_plane[:, g, cols]
+        def multiply(h, i, product, g, c0, c1, acc):
+            filters = slice(i * P, (i + 1) * P)
+            if product == "z":
+                codes, plane = gate_codes[g][:, filters].bitcast(FP8X4), gate_plane[g][:, filters]
+            elif product == "fast":
+                codes, plane = band_codes[g][:, filters].bitcast(FP8X4), band_plane[:, g, filters]
             else:
-                weights, plane = low_codes[:, g, 2 * nt * P : 2 * (nt + 1) * P].bitcast(FP4X4), low_plane[:, g, cols]
+                codes, plane = low_codes[:, g, 2 * i * P : 2 * (i + 1) * P].bitcast(FP4X4), low_plane[:, g, filters]
             nc.tensor.matmul_mx(
-                out=acc, lhsT=weights, lhsT_scale=plane,
+                out=acc, lhsT=codes, lhsT_scale=plane,
                 rhs=a_codes[h, g][:, c0:c1].bitcast(FP8X4), rhs_scale=a_plane[h, g][:, c0:c1],
-                start=(g == 0), stop=(g == PASSES - 1),
+                start=(g == 0), stop=(g == LAST_PASS),
             )
 
-        def gate_and_band_pass(h, g, c0, c1, kinds=("z", "fast")):
-            for kind in kinds:
-                for nt in range(NT):
+        def bank_of(h, i, product):
+            return i + TILES * ((h + (product == "fast")) % 2)
+
+        def gate_and_band_pass(h, g, c0):
+            for product in ("z", "fast"):
+                for i in range(TILES):
                     if g == 0 and c0 == 0:
-                        open_bank((h, nt, kind), (nt + (4 if (kind == "fast") != (h == 1) else 0)))
-                    multiply(h, nt, kind, g, c0, c1, sums[h, nt, kind][:, c0:c1])
+                        open_bank((h, i, product), bank_of(h, i, product))
+                    multiply(h, i, product, g, c0, c0 + STAGE, sums[h, i, product][:, c0 : c0 + STAGE])
 
-        def slow_group(h, nt, c0, c1, bank):
-            open_bank((h, nt, "slow", c0), bank)
+        def slow_group(h, i, c0, c1, bank):
+            open_bank((h, i, "slow", c0), bank)
             for g in range(PASSES):
-                multiply(h, nt, "slow", g, c0, c1, sums[h, nt, "slow", c0][:, : c1 - c0])
+                multiply(h, i, "slow", g, c0, c1, sums[h, i, "slow", c0][:, : c1 - c0])
 
-        def make_a(h, g, c0, c1):
-            mid = (c0 + c1) // 2
-            take_exp(h, g, c0, mid)
-            group_a(h, g, c0, mid)
-            take_exp(h, g, mid, c1)
-            group_a(h, g, mid, c1)
-            quantize_a(h, g, c0, mid)
-            quantize_a(h, g, mid, c1)
-
-        tanhs = {}
+        gains = {}
         gated = {}
 
-        def take_tanh(h, nt):
-            tanhs[h, nt] = work.tile([P, HALF], F32, name="tanh", bufs=4)
+        def take_gain(h, i):
+            gains[h, i] = work.tile([P, HALF], F32, name="gain", bufs=TILES)
             nc.scalar.activation(
-                out=tanhs[h, nt][:], in_=sums[h, nt, "z"][:], func=ACT.Sigmoid, bias=bias_sb[:, nt, 0:1],
+                out=gains[h, i][:], in_=sums[h, i, "z"][:], func=ACT.Sigmoid, bias=bias_sb[:, i, 0:1],
             )
 
-        def apply_gain(h, nt):
-            gated[h, nt] = work.tile([P, HALF], F32, name="gated", bufs=4)
-            nc.vector.tensor_tensor(
-                out=gated[h, nt][:], in0=tanhs[h, nt][:], in1=sums[h, nt, "fast"][:], op=ALU.mult
-            )
+        def apply_gain(h, i):
+            gated[h, i] = work.tile([P, HALF], F32, name="gated", bufs=TILES)
+            nc.vector.tensor_tensor(out=gated[h, i][:], in0=gains[h, i][:], in1=sums[h, i, "fast"][:], op=ALU.mult)
 
-        def finish(h, nt, c0, c1, queue):
+        def finish(h, i, c0, c1, queue):
             result = work.tile([P, c1 - c0], F32, name="result", bufs=8)
             nc.vector.tensor_tensor(
-                out=result[:], in0=gated[h, nt][:, c0:c1], in1=sums[h, nt, "slow", c0][:, : c1 - c0], op=ALU.add
+                out=result[:], in0=gated[h, i][:, c0:c1], in1=sums[h, i, "slow", c0][:, : c1 - c0], op=ALU.add
             )
-            queue.dma_start(out=out[nt * P : (nt + 1) * P, h * HALF + c0 : h * HALF + c1], in_=result[:])
+            queue.dma_start(out=out[i * P : (i + 1) * P, h * HALF + c0 : h * HALF + c1], in_=result[:])
 
-        nc.scalar.dma_start(out=taper_sb[:], in_=taper.rearrange("(g p j) -> p g j", p=P, j=PACK))
-        nc.vector.memset(ones[:], 1.0)
-        nc.vector.memset(shift[:], -SHIFT)
-        nc.scalar.activation(out=warm[:], in_=ones[:], func=ACT.Ln)
+        nc.scalar.dma_start(out=taper_sb[:], in_=taper.rearrange("(g p t) -> p g t", p=P, t=PACK))
+        nc.vector.memset(minus_shift[:], -SHIFT)
         nc.gpsimd.memset(band_plane[:].bitcast(I32), 0)
         nc.gpsimd.memset(low_plane[:].bitcast(I32), 0)
-        for piece in range(5):
-            load_energy(0, piece)
+        for i in range(len(pieces[0])):
+            load_energy(0, i)
         load_energy(1, 0)
         load_energy(1, 1)
         load_gate(0)
@@ -243,9 +235,9 @@ def tile_gammatone_modulation_filters_s10_kernel(
         nc.sync.dma_start(out=low_codes[:].bitcast(I32), in_=low_words.rearrange("g p n -> p g n").bitcast(I32))
         load_plane(low_plane, low_scales)
         with nc.allow_non_contiguous_dma(reason="one bias value a partition"):
-            nc.sync.dma_start(out=bias_sb[:, :, 0], in_=bias.rearrange("(t p) -> p t", p=P))
+            nc.sync.dma_start(out=bias_sb[:, :, 0], in_=bias.rearrange("(i p) -> p i", p=P))
 
-        nc.vector.tensor_copy(out=taper_f32[:], in_=taper_sb[:].rearrange("p g j -> p (g j)"))
+        nc.vector.tensor_copy(out=taper_f32[:], in_=taper_sb[:].rearrange("p g t -> p (g t)"))
         nc.vector.tensor_scalar(
             out=taper_mantissa[:], in0=taper_f32[:].bitcast(I32), scalar1=MANTISSA, scalar2=ONE_BITS,
             op0=ALU.bitwise_and, op1=ALU.bitwise_or,
@@ -260,92 +252,86 @@ def tile_gammatone_modulation_filters_s10_kernel(
             op0=ALU.mult, op1=ALU.mult,
         )
         nc.vector.tensor_scalar(
-            out=taper_sign[:].rearrange("p g j -> p (g j)"), in0=taper_power[:].bitcast(F32),
+            out=taper_factor[:].rearrange("p g t -> p (g t)"), in0=taper_power[:].bitcast(F32),
             scalar1=2.0**SHIFT_BITS, scalar2=None, op0=ALU.mult,
         )
-
         nc.vector.tensor_tensor(out=taper_cube[:], in0=taper_square[:], in1=mantissa, op=ALU.mult)
 
-        for piece in range(4):
-            take_log(0, piece)
+        for i in range(len(pieces[0]) - 1):
+            take_plain_log(0, i)
         nc.scalar.activation(out=taper_log[:], in_=taper_cube[:], func=ACT.Ln)
-        take_log(0, 4)
-        for j in range(PACK):
-            add_taper_log(0, j)
+        take_plain_log(0, len(pieces[0]) - 1)
+        for t in range(PACK):
+            add_taper_log(0, t)
         for g in range(1, PASSES):
-            take_scaled_logs(g, 0)
-            take_scaled_logs(g, 1)
+            for i in range(len(pieces[g])):
+                take_tapered_logs(g, i)
         for g in range(PASSES):
-            group_gate(g)
-            if g == PASSES - 1:
+            interleave_gate(g)
+            if g == LAST_PASS:
                 add_taper_log(*LATE_ROW)
             quantize_gate(g)
-        scratch = psum.tile([P, HALF], F32, name="bank7")
+
+        unread = psum.tile([P, HALF], F32, name="bank%d" % bank_of(0, LAST_TILE, "fast"))
         for i in range(WARM_UPS):
             nc.tensor.matmul_mx(
-                out=scratch[:], lhsT=gate_codes[3][:, :P].bitcast(FP8X4), lhsT_scale=gate_plane[3][:, :P],
-                rhs=gate_codes[3][:].bitcast(FP8X4), rhs_scale=gate_plane[3][:], start=True, stop=True,
+                out=unread[:],
+                lhsT=gate_codes[LAST_PASS][:, :P].bitcast(FP8X4), lhsT_scale=gate_plane[LAST_PASS][:, :P],
+                rhs=gate_codes[LAST_PASS][:].bitcast(FP8X4), rhs_scale=gate_plane[LAST_PASS][:],
+                start=True, stop=True,
             )
 
-        for c0 in (0, 256):
+        for c0 in (0, STAGE):
             for g in range(PASSES):
-                make_a(0, g, c0, c0 + 256)
-                gate_and_band_pass(0, g, c0, c0 + 256)
+                parts = [(c0, c0 + STAGE // 2), (c0 + STAGE // 2, c0 + STAGE)]
+                for part in parts:
+                    take_roots(0, g, *part)
+                    pack_a(0, g, *part)
+                for part in parts:
+                    quantize_a(0, g, *part)
+                gate_and_band_pass(0, g, c0)
 
-        take_exp(1, 0, 0, 256)
-        group_a(1, 0, 0, 256)
-        take_tanh(0, 0)
-        slow_group(0, 0, 0, HALF, 0)
-        take_tanh(0, 1)
-        slow_group(0, 1, 0, HALF, 1)
+        take_roots(1, 0, 0, STAGE)
+        pack_a(1, 0, 0, STAGE)
+        for i in (0, 1):
+            take_gain(0, i)
+            slow_group(0, i, 0, HALF, bank_of(0, i, "slow"))
         apply_gain(0, 0)
-        quantize_a(1, 0, 0, 256)
+        quantize_a(1, 0, 0, STAGE)
         apply_gain(0, 1)
         finish(0, 0, 0, HALF, nc.sync)
-        take_tanh(0, 2)
-        slow_group(0, 2, 0, HALF, 2)
-        take_exp(1, 1, 0, 256)
-        take_tanh(0, 3)
-        slow_group(0, 3, 0, HALF, 3)
-        apply_gain(0, 2)
-        finish(0, 1, 0, HALF, nc.sync)
-        apply_gain(0, 3)
-        finish(0, 2, 0, HALF, nc.sync)
-        group_a(1, 1, 0, 256)
+        take_gain(0, 2)
+        slow_group(0, 2, 0, HALF, bank_of(0, 2, "slow"))
+        take_roots(1, 1, 0, STAGE)
+        take_gain(0, 3)
+        slow_group(0, 3, 0, HALF, bank_of(0, 3, "slow"))
+        for i in (2, 3):
+            apply_gain(0, i)
+            finish(0, i - 1, 0, HALF, nc.sync)
+        pack_a(1, 1, 0, STAGE)
         finish(0, 3, 0, HALF, nc.sync)
-        quantize_a(1, 1, 0, 256)
-        gate_and_band_pass(1, 0, 0, 256)
-        gate_and_band_pass(1, 1, 0, 256)
-        take_exp(1, 2, 0, 256)
-        group_a(1, 2, 0, 256)
-        take_exp(1, 3, 0, 256)
-        group_a(1, 3, 0, 256)
-        quantize_a(1, 2, 0, 256)
-        gate_and_band_pass(1, 2, 0, 256)
-        take_exp(1, 0, 256, 512)
-        group_a(1, 0, 256, 512)
-        quantize_a(1, 3, 0, 256)
-        gate_and_band_pass(1, 3, 0, 256)
-        take_exp(1, 1, 256, 512)
-        group_a(1, 1, 256, 512)
-        quantize_a(1, 0, 256, 512)
-        gate_and_band_pass(1, 0, 256, 512)
-        take_exp(1, 2, 256, 512)
-        group_a(1, 2, 256, 512)
-        quantize_a(1, 1, 256, 512)
-        gate_and_band_pass(1, 1, 256, 512)
-        take_exp(1, 3, 256, 512)
-        group_a(1, 3, 256, 512)
-        quantize_a(1, 2, 256, 512)
-        gate_and_band_pass(1, 2, 256, 512)
-        quantize_a(1, 3, 256, 512)
-        gate_and_band_pass(1, 3, 256, 512)
-        for nt in range(NT):
-            take_tanh(1, nt)
-            apply_gain(1, nt)
-        for nt in range(NT - 1):
-            slow_group(1, nt, 0, HALF, 4 + nt)
-            finish(1, nt, 0, HALF, nc.sync)
-        for i, bank in enumerate((7, 0, 1, 2)):
-            slow_group(1, NT - 1, i * P, (i + 1) * P, bank)
-            finish(1, NT - 1, i * P, (i + 1) * P, nc.scalar if i % 2 else nc.sync)
+        quantize_a(1, 1, 0, STAGE)
+        gate_and_band_pass(1, 0, 0)
+        gate_and_band_pass(1, 1, 0)
+
+        rest = [(g, c0) for c0 in (0, STAGE) for g in range(PASSES)][2:]
+        for step in range(len(rest) + 1):
+            if step < len(rest):
+                g, c0 = rest[step]
+                take_roots(1, g, c0, c0 + STAGE)
+                pack_a(1, g, c0, c0 + STAGE)
+            if step > 0:
+                g, c0 = rest[step - 1]
+                quantize_a(1, g, c0, c0 + STAGE)
+                gate_and_band_pass(1, g, c0)
+
+        for i in range(TILES):
+            take_gain(1, i)
+            apply_gain(1, i)
+        for i in range(LAST_TILE):
+            slow_group(1, i, 0, HALF, bank_of(1, i, "slow"))
+            finish(1, i, 0, HALF, nc.sync)
+        banks = [bank_of(1, LAST_TILE, "slow")] + [bank_of(1, i, "fast") for i in range(LAST_TILE)]
+        for j, bank in enumerate(banks):
+            slow_group(1, LAST_TILE, j * P, (j + 1) * P, bank)
+            finish(1, LAST_TILE, j * P, (j + 1) * P, nc.scalar if j % 2 else nc.sync)

import math
from contextlib import ExitStack

import concourse.mybir as mybir

K, C, N = 2048, 1024, 512
FLOPS = 3 * 2 * K * C * N

F32 = mybir.dt.float32
BF16 = mybir.dt.bfloat16
I32 = mybir.dt.int32
U32 = mybir.dt.uint32
U8 = mybir.dt.uint8
FP8X4 = mybir.dt.float8_e4m3fn_x4
FP4X4 = mybir.dt.float4_e2m1fn_x4
ACT = mybir.ActivationFunctionType
ALU = mybir.AluOpType

P = 128
PACK = 4
PASSES = K // (P * PACK)
LAST_PASS = PASSES - 1
HALF = 512
HALVES = C // HALF
STAGE = HALF // 2
TILES = N // P
LAST_TILE = TILES - 1

SHIFT = 30.0
SHIFT_BITS = 43
SIGN_AND_EXPONENT = -(1 << 23)
MANTISSA = (1 << 23) - 1
ONE_BITS = 127 << 23

WARM_UPS = 6
LATE_ROW = (LAST_PASS, PACK - 2)


def tile_gammatone_modulation_filters_s10_kernel(
    tc, energy, taper, low_words, low_scales, band_words, band_scales, gate, bias, out
):
    nc = tc.nc
    with ExitStack() as ctx:
        keep = ctx.enter_context(tc.tile_pool(name="keep", bufs=1))
        work = ctx.enter_context(tc.tile_pool(name="work", bufs=3))
        psum = ctx.enter_context(tc.psum_pool(name="psum", bufs=1))
        ctx.enter_context(tc.manual_schedule())

        def kept(shape, dtype, name):
            return keep.tile(shape, dtype, name=name, align_bytes=64)

        energy_rows = energy.rearrange("(g p t) c -> g p t c", p=P, t=PACK)
        gate_rows = gate.rearrange("(g p t) n -> g p t n", p=P, t=PACK)

        pieces = [[(0, 1, 0, HALF), (0, 1, HALF, C)] + [(t, t + 1, 0, C) for t in range(1, PACK)]]
        pieces += [[(0, 2, 0, C), (2, 4, 0, C)]] * (PASSES - 1)
        energy_sb = {}
        for g in range(PASSES):
            for i, (t0, t1, c0, c1) in enumerate(pieces[g]):
                energy_sb[g, i] = kept([P, t1 - t0, c1 - c0], BF16, "energy%d_%d" % (g, i))
        logs = [kept([P, PACK, C], F32, "logs%d" % g) for g in range(PASSES)]
        gate_sb = [kept([P, PACK, N], BF16, "gate%d" % g) for g in range(PASSES)]
        gate_codes = [kept([P, N], U32, "gate_codes%d" % g) for g in range(PASSES)]
        gate_plane = [kept([P, N], U8, "gate_plane%d" % g) for g in range(PASSES)]
        band_codes = [kept([P, N], U32, "band_codes%d" % g) for g in range(PASSES)]
        low_codes = kept([P, PASSES, 2 * N], U8, "low_codes")
        band_plane = kept([P, PASSES, N], U8, "band_plane")
        low_plane = kept([P, PASSES, N], U8, "low_plane")
        a_codes = {}
        a_plane = {}
        for h in range(HALVES):
            for g in range(PASSES):
                a_codes[h, g] = kept([P, HALF], U32, "a_codes%d_%d" % (h, g))
                a_plane[h, g] = kept([P, HALF], U8, "a_plane%d_%d" % (h, g))
        taper_sb = kept([P, PASSES, PACK], BF16, "taper_sb")
        taper_f32 = kept([P, PASSES * PACK], F32, "taper_f32")
        taper_power = kept([P, PASSES * PACK], I32, "taper_power")
        taper_mantissa = kept([P, PASSES * PACK], I32, "taper_mantissa")
        minus_shift = kept([P, 1], F32, "minus_shift")
        taper_square = kept([P, PASSES * PACK], F32, "taper_square")
        taper_cube = kept([P, PASSES * PACK], F32, "taper_cube")
        taper_log = kept([P, PASSES * PACK], F32, "taper_log")
        taper_factor = kept([P, PASSES, PACK], BF16, "taper_factor")
        bias_sb = kept([P, TILES, 2], BF16, "bias_sb")

        def load_energy(g, i):
            t0, t1, c0, c1 = pieces[g][i]
            nc.sync.dma_start(out=energy_sb[g, i][:], in_=energy_rows[g][:, t0:t1, c0:c1])

        def load_gate(g):
            nc.sync.dma_start(out=gate_sb[g][:], in_=gate_rows[g])

        def load_plane(plane, scales):
            rows = scales.bitcast(I32).rearrange("g (q r) n -> r q g n", r=4)
            for r in range(4):
                nc.sync.dma_start(out=plane[:].bitcast(I32)[r:P:32], in_=rows[r])

        def take_plain_log(g, i):
            t0, t1, c0, c1 = pieces[g][i]
            nc.scalar.activation(out=logs[g][:, t0:t1, c0:c1], in_=energy_sb[g, i][:], func=ACT.Ln)

        def take_tapered_logs(g, i):
            t0, t1 = pieces[g][i][:2]
            for t in range(t0, t1):
                col = g * PACK + t
                nc.scalar.activation(
                    out=logs[g][:, t, :], in_=energy_sb[g, i][:, t - t0, :], func=ACT.Ln,
                    scale=1.0 if (g, t) == LATE_ROW else taper_cube[:, col : col + 1],
                )

        def add_taper_log(g, t):
            col = g * PACK + t
            nc.vector.tensor_scalar(
                out=logs[g][:, t, :], in0=logs[g][:, t, :], scalar1=taper_log[:, col : col + 1], scalar2=None,
                op0=ALU.add,
            )

        gate_packed = {}

        def interleave_gate(g):
            gate_packed[g] = work.tile([P, N, PACK], BF16, name="gate_packed", bufs=2, align_bytes=64)
            nc.vector.tensor_copy(
                out=gate_packed[g][:].rearrange("p (n i) t -> p n t i", i=4),
                in_=gate_sb[g][:].rearrange("p t (n i) -> p n t i", i=4),
            )

        def quantize_gate(g):
            nc.vector.quantize_mx(
                out=gate_codes[g][:].bitcast(FP8X4), scales=gate_plane[g][:],
                in_=gate_packed[g][:].rearrange("p n t -> p (n t)"),
            )

        roots = {}
        a_packed = {}

        def take_roots(h, g, c0, c1):
            roots[h, g, c0] = work.tile([P, 2, c1 - c0, 2], BF16, name="roots", bufs=4, align_bytes=64)
            nc.scalar.activation(
                out=roots[h, g, c0][:],
                in_=logs[g][:, :, h * HALF + c0 : h * HALF + c1].rearrange("p (u e) c -> p u c e", e=2),
                func=ACT.Sigmoid, bias=minus_shift[:], scale=1.0 / 3.0,
            )

        def pack_a(h, g, c0, c1):
            a_packed[h, g, c0] = work.tile([P, c1 - c0, PACK], BF16, name="a_packed", bufs=4, align_bytes=64)
            factor = taper_factor[:, g, :].rearrange("p (u e) -> p u e", e=2)
            nc.vector.tensor_tensor(
                out=a_packed[h, g, c0][:].rearrange("p c (u e) -> p c u e", e=2),
                in0=roots[h, g, c0][:].rearrange("p u c e -> p c u e"),
                in1=factor.unsqueeze(1).to_broadcast([P, c1 - c0, 2, 2]),
                op=ALU.mult,
            )

        def quantize_a(h, g, c0, c1):
            nc.vector.quantize_mx(
                out=a_codes[h, g][:, c0:c1].bitcast(FP8X4), scales=a_plane[h, g][:, c0:c1],
                in_=a_packed[h, g, c0][:].rearrange("p c t -> p (c t)"),
            )

        sums = {}

        def open_bank(key, bank):
            sums[key] = psum.tile([P, HALF], F32, name="bank%d" % bank)

        def multiply(h, i, product, g, c0, c1, acc):
            filters = slice(i * P, (i + 1) * P)
            if product == "z":
                codes, plane = gate_codes[g][:, filters].bitcast(FP8X4), gate_plane[g][:, filters]
            elif product == "fast":
                codes, plane = band_codes[g][:, filters].bitcast(FP8X4), band_plane[:, g, filters]
            else:
                codes, plane = low_codes[:, g, 2 * i * P : 2 * (i + 1) * P].bitcast(FP4X4), low_plane[:, g, filters]
            nc.tensor.matmul_mx(
                out=acc, lhsT=codes, lhsT_scale=plane,
                rhs=a_codes[h, g][:, c0:c1].bitcast(FP8X4), rhs_scale=a_plane[h, g][:, c0:c1],
                start=(g == 0), stop=(g == LAST_PASS),
            )

        def bank_of(h, i, product):
            return i + TILES * ((h + (product == "fast")) % 2)

        def gate_and_band_pass(h, g, c0):
            for product in ("z", "fast"):
                for i in range(TILES):
                    if g == 0 and c0 == 0:
                        open_bank((h, i, product), bank_of(h, i, product))
                    multiply(h, i, product, g, c0, c0 + STAGE, sums[h, i, product][:, c0 : c0 + STAGE])

        def slow_group(h, i, c0, c1, bank):
            open_bank((h, i, "slow", c0), bank)
            for g in range(PASSES):
                multiply(h, i, "slow", g, c0, c1, sums[h, i, "slow", c0][:, : c1 - c0])

        gains = {}
        gated = {}

        def take_gain(h, i):
            gains[h, i] = work.tile([P, HALF], F32, name="gain", bufs=TILES)
            nc.scalar.activation(
                out=gains[h, i][:], in_=sums[h, i, "z"][:], func=ACT.Sigmoid, bias=bias_sb[:, i, 0:1],
            )

        def apply_gain(h, i):
            gated[h, i] = work.tile([P, HALF], F32, name="gated", bufs=TILES)
            nc.vector.tensor_tensor(out=gated[h, i][:], in0=gains[h, i][:], in1=sums[h, i, "fast"][:], op=ALU.mult)

        def finish(h, i, c0, c1, queue):
            result = work.tile([P, c1 - c0], F32, name="result", bufs=8)
            nc.vector.tensor_tensor(
                out=result[:], in0=gated[h, i][:, c0:c1], in1=sums[h, i, "slow", c0][:, : c1 - c0], op=ALU.add
            )
            queue.dma_start(out=out[i * P : (i + 1) * P, h * HALF + c0 : h * HALF + c1], in_=result[:])

        nc.scalar.dma_start(out=taper_sb[:], in_=taper.rearrange("(g p t) -> p g t", p=P, t=PACK))
        nc.vector.memset(minus_shift[:], -SHIFT)
        nc.gpsimd.memset(band_plane[:].bitcast(I32), 0)
        nc.gpsimd.memset(low_plane[:].bitcast(I32), 0)
        for i in range(len(pieces[0])):
            load_energy(0, i)
        load_energy(1, 0)
        load_energy(1, 1)
        load_gate(0)
        load_energy(2, 0)
        load_gate(1)
        load_energy(2, 1)
        load_energy(3, 0)
        load_gate(2)
        load_energy(3, 1)
        load_gate(3)
        load_plane(band_plane, band_scales)
        for g in range(PASSES):
            nc.sync.dma_start(
                out=band_codes[g][:].bitcast(I32), in_=band_words[g].rearrange("p n t -> p (n t)").bitcast(I32)
            )
        nc.sync.dma_start(out=low_codes[:].bitcast(I32), in_=low_words.rearrange("g p n -> p g n").bitcast(I32))
        load_plane(low_plane, low_scales)
        with nc.allow_non_contiguous_dma(reason="one bias value a partition"):
            nc.sync.dma_start(out=bias_sb[:, :, 0], in_=bias.rearrange("(i p) -> p i", p=P))

        nc.vector.tensor_copy(out=taper_f32[:], in_=taper_sb[:].rearrange("p g t -> p (g t)"))
        nc.vector.tensor_scalar(
            out=taper_mantissa[:], in0=taper_f32[:].bitcast(I32), scalar1=MANTISSA, scalar2=ONE_BITS,
            op0=ALU.bitwise_and, op1=ALU.bitwise_or,
        )
        nc.vector.tensor_scalar(
            out=taper_power[:], in0=taper_f32[:].bitcast(I32), scalar1=SIGN_AND_EXPONENT, scalar2=None,
            op0=ALU.bitwise_and,
        )
        mantissa = taper_mantissa[:].bitcast(F32)
        nc.vector.scalar_tensor_tensor(
            out=taper_square[:], in0=mantissa, scalar=(math.e**SHIFT / 2.0**SHIFT_BITS) ** 3, in1=mantissa,
            op0=ALU.mult, op1=ALU.mult,
        )
        nc.vector.tensor_scalar(
            out=taper_factor[:].rearrange("p g t -> p (g t)"), in0=taper_power[:].bitcast(F32),
            scalar1=2.0**SHIFT_BITS, scalar2=None, op0=ALU.mult,
        )
        nc.vector.tensor_tensor(out=taper_cube[:], in0=taper_square[:], in1=mantissa, op=ALU.mult)

        for i in range(len(pieces[0]) - 1):
            take_plain_log(0, i)
        nc.scalar.activation(out=taper_log[:], in_=taper_cube[:], func=ACT.Ln)
        take_plain_log(0, len(pieces[0]) - 1)
        for t in range(PACK):
            add_taper_log(0, t)
        for g in range(1, PASSES):
            for i in range(len(pieces[g])):
                take_tapered_logs(g, i)
        for g in range(PASSES):
            interleave_gate(g)
            if g == LAST_PASS:
                add_taper_log(*LATE_ROW)
            quantize_gate(g)

        unread = psum.tile([P, HALF], F32, name="bank%d" % bank_of(0, LAST_TILE, "fast"))
        for i in range(WARM_UPS):
            nc.tensor.matmul_mx(
                out=unread[:],
                lhsT=gate_codes[LAST_PASS][:, :P].bitcast(FP8X4), lhsT_scale=gate_plane[LAST_PASS][:, :P],
                rhs=gate_codes[LAST_PASS][:].bitcast(FP8X4), rhs_scale=gate_plane[LAST_PASS][:],
                start=True, stop=True,
            )

        for c0 in (0, STAGE):
            for g in range(PASSES):
                parts = [(c0, c0 + STAGE // 2), (c0 + STAGE // 2, c0 + STAGE)]
                for part in parts:
                    take_roots(0, g, *part)
                    pack_a(0, g, *part)
                for part in parts:
                    quantize_a(0, g, *part)
                gate_and_band_pass(0, g, c0)

        take_roots(1, 0, 0, STAGE)
        pack_a(1, 0, 0, STAGE)
        for i in (0, 1):
            take_gain(0, i)
            slow_group(0, i, 0, HALF, bank_of(0, i, "slow"))
        apply_gain(0, 0)
        quantize_a(1, 0, 0, STAGE)
        apply_gain(0, 1)
        finish(0, 0, 0, HALF, nc.sync)
        take_gain(0, 2)
        slow_group(0, 2, 0, HALF, bank_of(0, 2, "slow"))
        take_roots(1, 1, 0, STAGE)
        take_gain(0, 3)
        slow_group(0, 3, 0, HALF, bank_of(0, 3, "slow"))
        for i in (2, 3):
            apply_gain(0, i)
            finish(0, i - 1, 0, HALF, nc.sync)
        pack_a(1, 1, 0, STAGE)
        finish(0, 3, 0, HALF, nc.sync)
        quantize_a(1, 1, 0, STAGE)
        gate_and_band_pass(1, 0, 0)
        gate_and_band_pass(1, 1, 0)

        rest = [(g, c0) for c0 in (0, STAGE) for g in range(PASSES)][2:]
        for step in range(len(rest) + 1):
            if step < len(rest):
                g, c0 = rest[step]
                take_roots(1, g, c0, c0 + STAGE)
                pack_a(1, g, c0, c0 + STAGE)
            if step > 0:
                g, c0 = rest[step - 1]
                quantize_a(1, g, c0, c0 + STAGE)
                gate_and_band_pass(1, g, c0)

        for i in range(TILES):
            take_gain(1, i)
            apply_gain(1, i)
        for i in range(LAST_TILE):
            slow_group(1, i, 0, HALF, bank_of(1, i, "slow"))
            finish(1, i, 0, HALF, nc.sync)
        banks = [bank_of(1, LAST_TILE, "slow")] + [bank_of(1, i, "fast") for i in range(LAST_TILE)]
        for j, bank in enumerate(banks):
            slow_group(1, LAST_TILE, j * P, (j + 1) * P, bank)
            finish(1, LAST_TILE, j * P, (j + 1) * P, nc.scalar if j % 2 else nc.sync)
